import numpy as np
import ml_dtypes


def mxq(x, axis, fmt="e4m3"):
    dtype, down = {"e4m3": (ml_dtypes.float8_e4m3fn, 7), "e5m2": (ml_dtypes.float8_e5m2, 14)}[fmt]
    v = np.moveaxis(np.asarray(x, np.float32).astype(ml_dtypes.bfloat16).astype(np.float64), axis, -1)
    blocks = v.reshape(v.shape[:-1] + (-1, 32))
    amax = np.abs(blocks).max(-1, keepdims=True)
    byte = np.maximum(np.where(amax > 0, np.frexp(amax)[1] - 1 + 127, 0) - down, 1)
    scale = np.exp2(byte - 127.0)
    codes = (blocks / scale).astype(np.float32).astype(dtype).astype(np.float64)
    return np.moveaxis((codes * scale).reshape(v.shape), -1, axis)


WIDE = False


def mx_kscale(k):
    if not WIDE:
        return np.ones(k)
    levels = np.array([10, -10, 5, -5, 0])
    if k % 512:
        return np.exp2(np.random.permutation(np.resize(levels, k // 32))).repeat(32)
    a = np.empty((k // 512, 16))
    for p in range(k // 512):
        a[p, :8] = np.random.permutation(np.resize(levels, 8))
        for g in range(8):
            far = levels[np.abs(levels - a[p, g]) >= 10]
            a[p, g + 8] = far[np.random.randint(len(far))]
    return np.exp2(a.ravel()).repeat(32)


def f64(x):
    return np.asarray(x).astype(np.float64)


def striped(idx):
    return np.tile(idx.reshape(-1, 16).T, (8, 1)).astype(np.uint16)


def unstriped(offs):
    return offs[:16].T.reshape(-1).astype(np.int64)


def pack_weight(w):
    k, n = w.shape
    w = f64(np.asarray(w, np.float32).astype(ml_dtypes.bfloat16)).reshape(k // 32, 32, n)
    amax = np.abs(w).max(1)
    byte = np.clip(np.where(amax > 0, np.frexp(amax)[1] - 1 + 127 - 7, 1), 1, 254)
    scaled = (w * np.exp2(127.0 - byte)[:, None, :]).reshape(k, n).astype(np.float32)
    words = np.ascontiguousarray(scaled.reshape(k // 512, 128, 4, n).transpose(0, 1, 3, 2)).astype(ml_dtypes.float8_e4m3fn).view(np.uint8)
    return words, np.ascontiguousarray(byte.astype(np.uint8).reshape(k // 512, 16, n))


def unpack_weight(words, scales):
    g, p, n, _ = words.shape
    vals = np.ascontiguousarray(words).view(ml_dtypes.float8_e4m3fn).astype(np.float64) * np.repeat(np.exp2(scales.astype(np.float64) - 127.0), 8, axis=1)[..., None]
    return vals.transpose(0, 1, 3, 2).reshape(g * 512, n)


def sigmoid(v):
    return 1.0 / (1.0 + np.exp(-np.maximum(v, -700.0)))


K, T, S, N, V = 1024, 2048, 1024, 256, 256
P = 2 ** 7


def setup_inputs():
    n = np.random.standard_normal
    s = mx_kscale(K)[:, None]
    packed_xT = pack_weight(n((K, T)) * s)
    return {
        "x_words": packed_xT[0],
        "x_scales": packed_xT[1],
        "w1": (n((K, N)) / np.sqrt(K) / s).astype(np.float32),
        "w2": (n((K, N)) / np.sqrt(K) / s).astype(np.float32),
        "gam": (np.tile(np.random.uniform(0.6, 0.95, V), (P, 1))).astype(np.float32),
        "offs": striped(np.random.permutation(T)[:S]),
        "rk1": striped(np.random.randint(0, S, V)),
        "rk2": striped(np.random.randint(0, S, V)),
        "rk3": striped(np.random.randint(0, S, V)),
        "rk4": striped(np.random.randint(0, S, V)),
    }


def reference(x_words, x_scales, w1, w2, gam, offs, rk1, rk2, rk3, rk4):
    xq = unpack_weight(x_words, x_scales)[:, unstriped(offs)]
    ya = mxq(f64(w1), 0, "e4m3").T @ xq
    att = sigmoid(ya)
    ck0 = att[:, unstriped(rk1)]
    ys = mxq(f64(w2), 0, "e4m3").T @ xq
    sat = sigmoid(ys)
    ex0 = f64(gam)[:1] * (-1.0 * (ck0 * sat[:, unstriped(rk1)]) + 1.0)
    ck1 = ex0 * att[:, unstriped(rk2)]
    ex1 = (f64(gam)[:1] * ex0) * (-1.0 * (att[:, unstriped(rk2)] * sat[:, unstriped(rk2)]) + 1.0)
    ck2 = ex1 * att[:, unstriped(rk3)]
    ex2 = (f64(gam)[:1] * ex1) * (-1.0 * (att[:, unstriped(rk3)] * sat[:, unstriped(rk3)]) + 1.0)
    ck3 = ex2 * att[:, unstriped(rk4)]
    ex3 = (f64(gam)[:1] * ex2) * (-1.0 * (att[:, unstriped(rk4)] * sat[:, unstriped(rk4)]) + 1.0)
    return (ck0 + ck1 + ck2 + ck3) / (-1.0 * (0.5 * ex3) + 1.0)

@@ -1,0 +1,216 @@
+from contextlib import ExitStack
+
+import concourse.mybir as mybir
+
+F32 = mybir.dt.float32
+BF16 = mybir.dt.bfloat16
+I32 = mybir.dt.int32
+U32 = mybir.dt.uint32
+U16 = mybir.dt.uint16
+U8 = mybir.dt.uint8
+FP8X4 = mybir.dt.float8_e4m3fn_x4
+ACT = mybir.ActivationFunctionType
+ALU = mybir.AluOpType
+
+K, T, S, N, V = 1024, 2048, 1024, 256, 256
+P = 128
+PACK = 4
+PASSES = K // (P * PACK)
+BANK = 512
+HALVES = S // BANK
+TILES = N // P
+FLOPS = 2 * 2 * K * N * S
+
+CAST = (("sv", "sv"), ("sv", "sv"))
+EVAC = (("vv", "ss"), ("ss", "ss"))
+A_BY = "ss"
+S_BY = "vs"
+SLOT = (0, 2, 1, 3)
+
+
+def tile_picked_ydbnclk_sum_p_kernel(tc, x_words, x_scales, w1, w2, gam, offs, rk1, rk2, rk3, rk4, out):
+    nc = tc.nc
+    with ExitStack() as ctx:
+        lists = ctx.enter_context(tc.tile_pool(name="lists", bufs=1))
+        keep = ctx.enter_context(tc.tile_pool(name="keep", bufs=1))
+        psum = ctx.enter_context(tc.psum_pool(name="psum", bufs=1))
+
+        picks = lists.tile([P, S // 16], U16, name="picks")
+        nc.sync.dma_start(picks[:], offs)
+
+        scale_table = keep.tile([P, T], U8, name="scale_table", align_bytes=64)
+        nc.vector.memset(scale_table[:, : T // 2].bitcast(I32), 0)
+        nc.gpsimd.memset(scale_table[:, T // 2 :].bitcast(I32), 0)
+        g = keep.tile([P, V], F32, name="g")
+        nc.sync.dma_start(g[:], gam)
+        ranks = []
+
+        def load_rank(rk):
+            rank = lists.tile([P, V // 16], U16, name="rank%d" % len(ranks))
+            nc.sync.dma_start(rank[:], rk)
+            ranks.append(rank)
+
+        load_rank(rk1)
+        for q in range(4):
+            (nc.sync, nc.scalar)[q % 2].dma_start(
+                scale_table[32 * q : 32 * q + 8, :].bitcast(I32),
+                x_scales[:, 4 * q : 4 * q + 4, :].bitcast(I32),
+            )
+
+        word_table, raw = {}, {}
+
+        def load_words(o):
+            word_table[o] = keep.tile([P, T], I32, name="word_table%d" % o, align_bytes=64)
+            nc.sync.dma_start(word_table[o][:], x_words[o].rearrange("p n t -> p (n t)").bitcast(I32))
+
+        def load_weights(i, o, m):
+            raw[i, o, m] = keep.tile([P, PACK, P], F32, name="raw%d%d%d" % (i, o, m))
+            rows = (w1, w2)[i][512 * o : 512 * (o + 1), m * P : (m + 1) * P]
+            nc.sync.dma_start(raw[i, o, m][:], rows.rearrange("(p j) c -> p j c", j=PACK))
+
+        load_words(0)
+        load_weights(0, 0, 0)
+        load_weights(1, 0, 0)
+        load_words(1)
+        load_weights(0, 1, 0)
+        load_weights(1, 1, 0)
+        for rk in (rk2, rk3, rk4):
+            load_rank(rk)
+        for i in range(2):
+            for o in range(PASSES):
+                load_weights(i, o, 1)
+
+
+        x_scale = keep.tile([P, S], U8, name="x_scale", align_bytes=64)
+        nc.vector.tensor_copy(x_scale[:], scale_table[:].indirect(picks[:]))
+        x_code = {}
+        for o in range(PASSES):
+            for h in range(HALVES):
+                x_code[o, h] = keep.tile([P, BANK], U32, name="x_code%d%d" % (o, h), align_bytes=64)
+                nc.vector.tensor_copy(
+                    x_code[o, h][:],
+                    word_table[o][:].bitcast(U32).indirect(picks[:, h * BANK // 16 : (h + 1) * BANK // 16]),
+                )
+
+        grouped, w_code, w_scale, banks, tables = {}, {}, {}, {}, {}
+
+        def cast(i, o, m):
+            grouped[i, o, m] = keep.tile([P, P * PACK], BF16, name="grouped%d%d%d" % (i, o, m), align_bytes=64)
+            dst = grouped[i, o, m][:].rearrange("p (c i t) -> p c t i", i=4, t=PACK)
+            src = raw[i, o, m][:].rearrange("p t (c i) -> p c t i", i=4)
+            if CAST[i][o][m] == "v":
+                nc.vector.tensor_copy(dst, src)
+            else:
+                nc.scalar.copy(dst, src)
+
+        def quantize(i, o, m):
+            w_code[i, o, m] = keep.tile([P, P], U32, name="w_code%d%d%d" % (i, o, m), align_bytes=64)
+            w_scale[i, o, m] = keep.tile([P, P], U8, name="w_scale%d%d%d" % (i, o, m), align_bytes=64)
+            nc.vector.quantize_mx(out=w_code[i, o, m][:].bitcast(FP8X4), scales=w_scale[i, o, m][:], in_=grouped[i, o, m][:])
+
+        def multiply(i, o, m):
+            for h in range(HALVES):
+                if o == 0:
+                    banks[i, m, h] = psum.tile([P, BANK], F32, name="bank%d%d%d" % (i, m, h))
+                nc.tensor.matmul_mx(
+                    out=banks[i, m, h][:],
+                    lhsT=w_code[i, o, m][:].bitcast(FP8X4),
+                    lhsT_scale=w_scale[i, o, m][:],
+                    rhs=x_code[o, h][:].bitcast(FP8X4),
+                    rhs_scale=x_scale[4 * o : P, h * BANK : (h + 1) * BANK],
+                    start=(o == 0),
+                    stop=(o == PASSES - 1),
+                )
+
+        def evacuate(i, m):
+            tables[i, m] = keep.tile([P, S], F32, name="table%d%d" % (i, m))
+            by = (A_BY, S_BY)[i][m]
+            for h in range(HALVES):
+                dst = tables[i, m][:, h * BANK : (h + 1) * BANK]
+                if by == "v":
+                    nc.scalar.activation(dst, banks[i, m, h][:], ACT.Sigmoid)
+                elif EVAC[i][m][h] == "v":
+                    nc.vector.tensor_copy(dst, banks[i, m, h][:])
+                else:
+                    nc.scalar.copy(dst, banks[i, m, h][:])
+
+        att, sat, both = {}, {}, {}
+
+        def fetch_att(m):
+            att[m] = keep.tile([P, 4, V], F32, name="att%d" % m)
+            for r in range(4):
+                window = tables[0, m][:].indirect(ranks[r][:])
+                if A_BY[m] == "v":
+                    nc.vector.tensor_copy(att[m][:, SLOT[r], :], window)
+                else:
+                    nc.scalar.activation(att[m][:, SLOT[r], :], window, ACT.Sigmoid)
+
+        def fetch_sat(m):
+            both[m] = keep.tile([P, 4, V], F32, name="both%d" % m)
+            if S_BY[m] == "s":
+                sat[m] = keep.tile([P, 4, V], F32, name="sat%d" % m)
+            for r in range(4):
+                window = tables[1, m][:].indirect(ranks[r][:])
+                if S_BY[m] == "v":
+                    nc.vector.tensor_tensor(both[m][:, SLOT[r], :], window, att[m][:, SLOT[r], :], ALU.mult)
+                else:
+                    nc.scalar.activation(sat[m][:, SLOT[r], :], window, ACT.Sigmoid)
+                    nc.vector.tensor_tensor(both[m][:, SLOT[r], :], sat[m][:, SLOT[r], :], att[m][:, SLOT[r], :], ALU.mult)
+
+        clicks, square = {}, {}
+
+        def combine(m):
+            step = keep.tile([P, 4, V], F32, name="step%d" % m)
+            nc.vector.scalar_tensor_tensor(
+                step[:], both[m][:], 1.0, g[:].unsqueeze(1).to_broadcast([P, 4, V]), ALU.subtract, ALU.mult
+            )
+            pair = keep.tile([P, 2, V], F32, name="pair%d" % m)
+            nc.vector.tensor_tensor(pair[:], step[:, 0:2, :], step[:, 2:4, :], ALU.mult)
+            lost = keep.tile([P, 2, V], F32, name="lost%d" % m)
+            nc.vector.tensor_tensor(lost[:], step[:, 0:2, :], att[m][:, 2:4, :], ALU.mult)
+            last = keep.tile([P, V], F32, name="last%d" % m)
+            nc.vector.tensor_tensor(last[:], pair[:, 0, :], pair[:, 1, :], ALU.mult)
+            square[m] = keep.tile([P, V], F32, name="square%d" % m)
+            nc.scalar.activation(square[m][:], last[:], ACT.Square, bias=1.0, scale=-0.5)
+            half = keep.tile([P, 2, V], F32, name="half%d" % m)
+            nc.vector.tensor_tensor(half[:], att[m][:, 0:2, :], lost[:], ALU.subtract)
+            low = keep.tile([P, V], F32, name="low%d" % m)
+            nc.vector.tensor_tensor(low[:], half[:, 1, :], pair[:, 0, :], ALU.mult)
+            clicks[m] = keep.tile([P, V], F32, name="clicks%d" % m)
+            nc.vector.tensor_tensor(clicks[m][:], low[:], half[:, 0, :], ALU.add)
+
+        def clock(ap, name):
+            tick = keep.tile([P, 1], F32, name=name)
+            nc.gpsimd.tensor_copy(tick[:], ap)
+
+        def finish(m, tag):
+            inverse = keep.tile([P, V], F32, name="inverse%d" % m, tag=tag)
+            nc.scalar.activation(inverse[:], square[m][:], ACT.Abs_reciprocal_sqrt)
+            result = keep.tile([P, V], F32, name="result%d" % m)
+            nc.vector.tensor_tensor(result[:], clicks[m][:], inverse[:], ALU.mult)
+            nc.sync.dma_start(out[m * P : (m + 1) * P, :], result[:])
+
+        for o in range(PASSES):
+            for i in range(2):
+                cast(i, o, 0)
+            for i in range(2):
+                quantize(i, o, 0)
+                multiply(i, o, 0)
+        evacuate(0, 0)
+        evacuate(1, 0)
+        for i in range(2):
+            for o in range(PASSES):
+                cast(i, o, 1)
+            for o in range(PASSES):
+                quantize(i, o, 1)
+                multiply(i, o, 1)
+        fetch_att(0)
+        fetch_sat(0)
+        evacuate(0, 1)
+        evacuate(1, 1)
+        combine(0)
+        fetch_att(1)
+        fetch_sat(1)
+        combine(1)
+        finish(0, "table11")
+        finish(1, "inverse1")

@@ -21,12 +21,6 @@ HALVES = S // BANK
 TILES = N // P
 FLOPS = 2 * 2 * K * N * S
 
-CAST = (("sv", "sv"), ("sv", "sv"))
-EVAC = (("vv", "ss"), ("ss", "ss"))
-A_BY = "ss"
-S_BY = "vs"
-SLOT = (0, 2, 1, 3)
-
 
 def tile_picked_ydbnclk_sum_p_kernel(tc, x_words, x_scales, w1, w2, gam, offs, rk1, rk2, rk3, rk4, out):
     nc = tc.nc
@@ -41,64 +35,47 @@ def tile_picked_ydbnclk_sum_p_kernel(tc, x_words, x_scales, w1, w2, gam, offs, r
         scale_table = keep.tile([P, T], U8, name="scale_table", align_bytes=64)
         nc.vector.memset(scale_table[:, : T // 2].bitcast(I32), 0)
         nc.gpsimd.memset(scale_table[:, T // 2 :].bitcast(I32), 0)
+
+        def load_scales():
+            for q in range(4):
+                (nc.sync, nc.scalar, nc.sync, nc.scalar)[q].dma_start(
+                    scale_table[32 * q : 32 * q + 8, :].bitcast(I32),
+                    x_scales[:, 4 * q : 4 * q + 4, :].bitcast(I32),
+                )
+
+
+        word_table, raw, ranks = {}, {}, []
         g = keep.tile([P, V], F32, name="g")
-        nc.sync.dma_start(g[:], gam)
-        ranks = []
-
-        def load_rank(rk):
-            rank = lists.tile([P, V // 16], U16, name="rank%d" % len(ranks))
-            nc.sync.dma_start(rank[:], rk)
-            ranks.append(rank)
-
-        load_rank(rk1)
-        for q in range(4):
-            (nc.sync, nc.scalar)[q % 2].dma_start(
-                scale_table[32 * q : 32 * q + 8, :].bitcast(I32),
-                x_scales[:, 4 * q : 4 * q + 4, :].bitcast(I32),
-            )
-
-        word_table, raw = {}, {}
 
         def load_words(o):
             word_table[o] = keep.tile([P, T], I32, name="word_table%d" % o, align_bytes=64)
             nc.sync.dma_start(word_table[o][:], x_words[o].rearrange("p n t -> p (n t)").bitcast(I32))
 
         def load_weights(i, o, m):
-            raw[i, o, m] = keep.tile([P, PACK, P], F32, name="raw%d%d%d" % (i, o, m))
+            raw[i, o, m] = keep.tile([P, PACK, P], F32, name="raw%d%d%d" % (i, o, m), align_bytes=64)
             rows = (w1, w2)[i][512 * o : 512 * (o + 1), m * P : (m + 1) * P]
             nc.sync.dma_start(raw[i, o, m][:], rows.rearrange("(p j) c -> p j c", j=PACK))
 
-        load_words(0)
-        load_weights(0, 0, 0)
-        load_weights(1, 0, 0)
-        load_words(1)
-        load_weights(0, 1, 0)
-        load_weights(1, 1, 0)
-        for rk in (rk2, rk3, rk4):
-            load_rank(rk)
-        for i in range(2):
-            for o in range(PASSES):
-                load_weights(i, o, 1)
+        def load_rank(rk):
+            rank = lists.tile([P, V // 16], U16, name="rank%d" % len(ranks))
+            nc.sync.dma_start(rank[:], rk)
+            ranks.append(rank)
 
-
+        x_code, grouped, w_code, w_scale, banks, tables = {}, {}, {}, {}, {}, {}
         x_scale = keep.tile([P, S], U8, name="x_scale", align_bytes=64)
-        nc.vector.tensor_copy(x_scale[:], scale_table[:].indirect(picks[:]))
-        x_code = {}
-        for o in range(PASSES):
-            for h in range(HALVES):
-                x_code[o, h] = keep.tile([P, BANK], U32, name="x_code%d%d" % (o, h), align_bytes=64)
-                nc.vector.tensor_copy(
-                    x_code[o, h][:],
-                    word_table[o][:].bitcast(U32).indirect(picks[:, h * BANK // 16 : (h + 1) * BANK // 16]),
-                )
 
-        grouped, w_code, w_scale, banks, tables = {}, {}, {}, {}, {}
+        def pick_scales():
+            nc.vector.tensor_copy(x_scale[:], scale_table[:].indirect(picks[:]))
 
-        def cast(i, o, m):
+        def pick_words(o, a, b, tag):
+            x_code[o, a] = keep.tile([P, b - a], U32, name="x_code%d_%d" % (o, a), tag=tag, align_bytes=64)
+            nc.vector.tensor_copy(x_code[o, a][:], word_table[o][:].bitcast(U32).indirect(picks[:, a // 16 : b // 16]))
+
+        def cast(i, o, m, by):
             grouped[i, o, m] = keep.tile([P, P * PACK], BF16, name="grouped%d%d%d" % (i, o, m), align_bytes=64)
             dst = grouped[i, o, m][:].rearrange("p (c i t) -> p c t i", i=4, t=PACK)
             src = raw[i, o, m][:].rearrange("p t (c i) -> p c t i", i=4)
-            if CAST[i][o][m] == "v":
+            if by == "v":
                 nc.vector.tensor_copy(dst, src)
             else:
                 nc.scalar.copy(dst, src)
@@ -108,109 +85,204 @@ def tile_picked_ydbnclk_sum_p_kernel(tc, x_words, x_scales, w1, w2, gam, offs, r
             w_scale[i, o, m] = keep.tile([P, P], U8, name="w_scale%d%d%d" % (i, o, m), align_bytes=64)
             nc.vector.quantize_mx(out=w_code[i, o, m][:].bitcast(FP8X4), scales=w_scale[i, o, m][:], in_=grouped[i, o, m][:])
 
-        def multiply(i, o, m):
-            for h in range(HALVES):
-                if o == 0:
-                    banks[i, m, h] = psum.tile([P, BANK], F32, name="bank%d%d%d" % (i, m, h))
-                nc.tensor.matmul_mx(
-                    out=banks[i, m, h][:],
-                    lhsT=w_code[i, o, m][:].bitcast(FP8X4),
-                    lhsT_scale=w_scale[i, o, m][:],
-                    rhs=x_code[o, h][:].bitcast(FP8X4),
-                    rhs_scale=x_scale[4 * o : P, h * BANK : (h + 1) * BANK],
-                    start=(o == 0),
-                    stop=(o == PASSES - 1),
-                )
-
-        def evacuate(i, m):
-            tables[i, m] = keep.tile([P, S], F32, name="table%d%d" % (i, m))
-            by = (A_BY, S_BY)[i][m]
-            for h in range(HALVES):
-                dst = tables[i, m][:, h * BANK : (h + 1) * BANK]
-                if by == "v":
-                    nc.scalar.activation(dst, banks[i, m, h][:], ACT.Sigmoid)
-                elif EVAC[i][m][h] == "v":
-                    nc.vector.tensor_copy(dst, banks[i, m, h][:])
-                else:
-                    nc.scalar.copy(dst, banks[i, m, h][:])
-
-        att, sat, both = {}, {}, {}
-
-        def fetch_att(m):
-            att[m] = keep.tile([P, 4, V], F32, name="att%d" % m)
-            for r in range(4):
-                window = tables[0, m][:].indirect(ranks[r][:])
-                if A_BY[m] == "v":
-                    nc.vector.tensor_copy(att[m][:, SLOT[r], :], window)
-                else:
-                    nc.scalar.activation(att[m][:, SLOT[r], :], window, ACT.Sigmoid)
-
-        def fetch_sat(m):
-            both[m] = keep.tile([P, 4, V], F32, name="both%d" % m)
-            if S_BY[m] == "s":
-                sat[m] = keep.tile([P, 4, V], F32, name="sat%d" % m)
-            for r in range(4):
-                window = tables[1, m][:].indirect(ranks[r][:])
-                if S_BY[m] == "v":
-                    nc.vector.tensor_tensor(both[m][:, SLOT[r], :], window, att[m][:, SLOT[r], :], ALU.mult)
-                else:
-                    nc.scalar.activation(sat[m][:, SLOT[r], :], window, ACT.Sigmoid)
-                    nc.vector.tensor_tensor(both[m][:, SLOT[r], :], sat[m][:, SLOT[r], :], att[m][:, SLOT[r], :], ALU.mult)
-
-        clicks, square = {}, {}
-
-        def combine(m):
-            step = keep.tile([P, 4, V], F32, name="step%d" % m)
-            nc.vector.scalar_tensor_tensor(
-                step[:], both[m][:], 1.0, g[:].unsqueeze(1).to_broadcast([P, 4, V]), ALU.subtract, ALU.mult
+        def multiply(i, o, m, a, b, code, tag):
+            if o == 0:
+                banks[i, m, a] = psum.tile([P, b - a], F32, name="bank%d%d_%d" % (i, m, a), tag=tag)
+            nc.tensor.matmul_mx(
+                out=banks[i, m, a][:],
+                lhsT=w_code[i, o, m][:].bitcast(FP8X4),
+                lhsT_scale=w_scale[i, o, m][:],
+                rhs=x_code[o, code][:, a - code : b - code].bitcast(FP8X4),
+                rhs_scale=x_scale[4 * o : P, a:b],
+                start=(o == 0),
+                stop=(o == PASSES - 1),
             )
-            pair = keep.tile([P, 2, V], F32, name="pair%d" % m)
-            nc.vector.tensor_tensor(pair[:], step[:, 0:2, :], step[:, 2:4, :], ALU.mult)
-            lost = keep.tile([P, 2, V], F32, name="lost%d" % m)
-            nc.vector.tensor_tensor(lost[:], step[:, 0:2, :], att[m][:, 2:4, :], ALU.mult)
-            last = keep.tile([P, V], F32, name="last%d" % m)
-            nc.vector.tensor_tensor(last[:], pair[:, 0, :], pair[:, 1, :], ALU.mult)
-            square[m] = keep.tile([P, V], F32, name="square%d" % m)
-            nc.scalar.activation(square[m][:], last[:], ACT.Square, bias=1.0, scale=-0.5)
-            half = keep.tile([P, 2, V], F32, name="half%d" % m)
-            nc.vector.tensor_tensor(half[:], att[m][:, 0:2, :], lost[:], ALU.subtract)
-            low = keep.tile([P, V], F32, name="low%d" % m)
-            nc.vector.tensor_tensor(low[:], half[:, 1, :], pair[:, 0, :], ALU.mult)
-            clicks[m] = keep.tile([P, V], F32, name="clicks%d" % m)
-            nc.vector.tensor_tensor(clicks[m][:], low[:], half[:, 0, :], ALU.add)
+
+        def evacuate(i, m, a, b, by, tag=None):
+            if (i, m) not in tables:
+                tables[i, m] = keep.tile([P, S], F32, name="table%d%d" % (i, m), tag=tag or "table%d%d" % (i, m), align_bytes=64)
+            dst = tables[i, m][:, a:b]
+            if by == "sigmoid":
+                nc.scalar.activation(dst, banks[i, m, a][:], ACT.Sigmoid)
+            elif by == "v":
+                nc.vector.tensor_copy(dst, banks[i, m, a][:])
+            else:
+                nc.scalar.copy(dst, banks[i, m, a][:])
+
+        def row(name, count=1, tag=None):
+            return keep.tile([P, count, V], F32, name=name, tag=tag or name, align_bytes=64)
+
+        att = [row("att%d" % m, 4) for m in range(TILES)]
+        sat = [row("sat%d" % m, 4) for m in range(TILES)]
+        both = {}
+        step = [row("step%d" % m, 4) for m in range(TILES)]
+        pair = [row("pair%d" % m, 2) for m in range(TILES)]
+        lost = [[row("lost%d%d" % (m, d)) for d in range(2)] for m in range(TILES)]
+        half = [row("half%d" % m, 2) for m in range(TILES)]
+        last = [row("last%d" % m) for m in range(TILES)]
+        square = [row("square%d" % m) for m in range(TILES)]
+        low = [row("low%d" % m) for m in range(TILES)]
+        clicks = [row("clicks%d" % m) for m in range(TILES)]
+        inverse = {}
+
+        def fetch_att(m, r):
+            nc.scalar.activation(att[m][:, r, :], tables[0, m][:].indirect(ranks[r][:]), ACT.Sigmoid)
+
+        def fetch_sat(m, r):
+            nc.scalar.activation(sat[m][:, r, :], tables[1, m][:].indirect(ranks[r][:]), ACT.Sigmoid)
+
+        def both_tile(m, a, b, tag):
+            tile = row("both%d%d" % (m, a), b - a, tag)
+            both[m, a, b] = tile[:]
+            for r in range(a, b):
+                both[m, r] = tile[:, r - a, :]
+
+        def fetch_both(m, r):
+            nc.vector.tensor_tensor(both[m, r], tables[1, m][:].indirect(ranks[r][:]), att[m][:, r, :], ALU.mult)
+
+        def do_both(m, a, b):
+            nc.vector.tensor_tensor(both[m, a, b], sat[m][:, a:b, :], att[m][:, a:b, :], ALU.mult)
+
+        def do_step(m, a, b):
+            nc.vector.scalar_tensor_tensor(
+                step[m][:, a:b, :], both[m, a, b], 1.0, g[:].unsqueeze(1).to_broadcast([P, b - a, V]), ALU.subtract, ALU.mult
+            )
+
+        def warm_up(ap):
+            warm = keep.tile([P, 1], F32, name="warm")
+            nc.scalar.activation(warm[:], ap, ACT.Sigmoid)
+
+        def do_pair(m, d):
+            nc.vector.tensor_tensor(pair[m][:, d, :], step[m][:, 2 * d, :], step[m][:, 2 * d + 1, :], ALU.mult)
+
+        def do_lost(m, d):
+            nc.vector.tensor_tensor(lost[m][d][:, 0, :], step[m][:, 2 * d, :], att[m][:, 2 * d + 1, :], ALU.mult)
+
+        def do_half(m, d):
+            nc.vector.tensor_tensor(half[m][:, d, :], att[m][:, 2 * d, :], lost[m][d][:, 0, :], ALU.subtract)
+
+        def wide(fn_out, fn_a, fn_b, op):
+            nc.vector.tensor_tensor(fn_out, fn_a, fn_b, op)
+
+        def do_last(m):
+            nc.vector.tensor_tensor(last[m][:, 0, :], pair[m][:, 0, :], pair[m][:, 1, :], ALU.mult)
+            nc.scalar.activation(square[m][:], last[m][:], ACT.Square, bias=1.0, scale=-0.5)
+
+        def do_low(m):
+            nc.vector.tensor_tensor(low[m][:, 0, :], half[m][:, 1, :], pair[m][:, 0, :], ALU.mult)
+
+        def do_clicks(m):
+            nc.vector.tensor_tensor(clicks[m][:, 0, :], low[m][:, 0, :], half[m][:, 0, :], ALU.add)
+
+        def do_inverse(m, tag):
+            inverse[m] = row("inverse%d" % m, 1, tag)
+            nc.scalar.activation(inverse[m][:], square[m][:], ACT.Abs_reciprocal_sqrt)
+
+        def finish(m, queue, tag):
+            result = row("result%d" % m, 1, tag)
+            nc.vector.tensor_tensor(result[:], clicks[m][:], inverse[m][:], ALU.mult)
+            queue.dma_start(out[m * P : (m + 1) * P, :], result[:, 0, :])
 
         def clock(ap, name):
             tick = keep.tile([P, 1], F32, name=name)
             nc.gpsimd.tensor_copy(tick[:], ap)
 
-        def finish(m, tag):
-            inverse = keep.tile([P, V], F32, name="inverse%d" % m, tag=tag)
-            nc.scalar.activation(inverse[:], square[m][:], ACT.Abs_reciprocal_sqrt)
-            result = keep.tile([P, V], F32, name="result%d" % m)
-            nc.vector.tensor_tensor(result[:], clicks[m][:], inverse[:], ALU.mult)
-            nc.sync.dma_start(out[m * P : (m + 1) * P, :], result[:])
-
-        for o in range(PASSES):
-            for i in range(2):
-                cast(i, o, 0)
-            for i in range(2):
-                quantize(i, o, 0)
-                multiply(i, o, 0)
-        evacuate(0, 0)
-        evacuate(1, 0)
+        load_weights(0, 0, 0)
+        load_scales()
+        load_words(0)
+        load_weights(1, 0, 0)
+        load_words(1)
+        load_weights(0, 1, 0)
+        load_weights(1, 1, 0)
+        for rk in (rk1, rk2, rk3, rk4):
+            load_rank(rk)
         for i in range(2):
             for o in range(PASSES):
-                cast(i, o, 1)
-            for o in range(PASSES):
-                quantize(i, o, 1)
-                multiply(i, o, 1)
-        fetch_att(0)
-        fetch_sat(0)
-        evacuate(0, 1)
-        evacuate(1, 1)
-        combine(0)
-        fetch_att(1)
-        fetch_sat(1)
-        combine(1)
-        finish(0, "table11")
-        finish(1, "inverse1")
+                load_weights(i, o, 1)
+        nc.sync.dma_start(g[:], gam)
+
+        warm_up(raw[0, 0, 0][:, 0, 0:1])
+        pick_scales()
+        pick_words(0, 0, 512, "x00")
+        pick_words(0, 512, 1024, "x01")
+        for o in range(PASSES):
+            for i in range(2):
+                cast(i, o, 0, "s")
+        quantize(0, 0, 0)
+        quantize(1, 0, 0)
+        pick_words(1, 0, 512, "x10")
+        quantize(0, 1, 0)
+        pick_words(1, 512, 768, "grouped010")
+        quantize(1, 1, 0)
+        pick_words(1, 768, 1024, "grouped110")
+        CUTS = ((0, 512), (512, 768), (768, 1024))
+        for i in range(2):
+            for a, b in CUTS:
+                multiply(i, 0, 0, a, b, a // 512 * 512, "bank%d_%d" % (i, a))
+        for a, b in CUTS:
+            for i in range(2):
+                multiply(i, 1, 0, a, b, a, None)
+        cast(0, 0, 1, "s")
+        cast(0, 1, 1, "s")
+        quantize(0, 0, 1)
+        cast(1, 0, 1, "v")
+        quantize(0, 1, 1)
+        for a, b in CUTS:
+            evacuate(0, 0, a, b, "v", "raw101")
+            evacuate(1, 0, a, b, "sigmoid", "raw011")
+        cast(1, 1, 1, "v")
+        quantize(1, 0, 1)
+        quantize(1, 1, 1)
+        for r in range(4):
+            fetch_att(0, r)
+        TAGS = (("fresh0", "bank0_0", "bank0_512"), ("fresh1", "bank1_0", "bank1_512"))
+        for i in range(2):
+            for c, (a, b) in enumerate(CUTS):
+                multiply(i, 0, 1, a, b, a // 512 * 512, TAGS[i][c])
+                multiply(i, 1, 1, a, b, a, None)
+        for i in range(2):
+            for a, b in CUTS:
+                evacuate(i, 1, a, b, "s")
+        both_tile(0, 0, 4, "grouped111")
+        both[0, 0, 2] = both[0, 0, 4][:, 0:2, :]
+        both[0, 2, 4] = both[0, 0, 4][:, 2:4, :]
+        fetch_both(0, 0)
+        fetch_both(0, 1)
+        fetch_both(0, 2)
+        do_step(0, 0, 2)
+        fetch_both(0, 3)
+        do_lost(0, 0)
+        do_step(0, 2, 4)
+        do_pair(0, 0)
+        do_half(0, 0)
+        do_lost(0, 1)
+        do_pair(0, 1)
+        do_half(0, 1)
+        do_last(0)
+        do_low(0)
+        for r in range(4):
+            fetch_att(1, r)
+            fetch_sat(1, r)
+        both_tile(1, 0, 2, "step0")
+        do_both(1, 0, 2)
+        do_clicks(0)
+        do_step(1, 0, 2)
+        both_tile(1, 2, 3, "step0")
+        do_both(1, 2, 3)
+        do_lost(1, 0)
+        do_pair(1, 0)
+        do_step(1, 2, 3)
+        do_half(1, 0)
+        both_tile(1, 3, 4, "lost10")
+        do_both(1, 3, 4)
+        do_lost(1, 1)
+        do_step(1, 3, 4)
+        do_inverse(0, "table11")
+        do_pair(1, 1)
+        do_half(1, 1)
+        do_last(1)
+        finish(0, nc.sync, "step1")
+        do_low(1)
+        do_clicks(1)
+        do_inverse(1, None)
+        finish(1, nc.sync, None)

@@ -15,10 +15,14 @@ ALU = mybir.AluOpType
 K, T, S, N, V = 1024, 2048, 1024, 256, 256
 P = 128
 PACK = 4
-PASSES = K // (P * PACK)
+K_PASS = P * PACK
+PASSES = K // K_PASS
+BLOCKS = N // P
+RANKS = 4
+LIST_ROWS = 16
+ATT, SAT = 0, 1
 BANK = 512
-HALVES = S // BANK
-TILES = N // P
+CUTS = ((0, BANK), (BANK, BANK + BANK // 2), (BANK + BANK // 2, S))
 FLOPS = 2 * 2 * K * N * S
 
 
@@ -29,23 +33,37 @@ def tile_picked_ydbnclk_sum_p_kernel(tc, x_words, x_scales, w1, w2, gam, offs, r
         keep = ctx.enter_context(tc.tile_pool(name="keep", bufs=1))
         psum = ctx.enter_context(tc.psum_pool(name="psum", bufs=1))
 
-        picks = lists.tile([P, S // 16], U16, name="picks")
+        picks = lists.tile([P, S // LIST_ROWS], U16, name="picks")
         nc.sync.dma_start(picks[:], offs)
 
         scale_table = keep.tile([P, T], U8, name="scale_table", align_bytes=64)
         nc.vector.memset(scale_table[:, : T // 2].bitcast(I32), 0)
         nc.gpsimd.memset(scale_table[:, T // 2 :].bitcast(I32), 0)
 
+        g = keep.tile([P, V], F32, name="g")
+        x_scale = keep.tile([P, S], U8, name="x_scale", align_bytes=64)
+        word_table, raw, ranks = {}, {}, []
+        x_code, grouped, w_code, w_scale, banks, tables = {}, {}, {}, {}, {}, {}
+
+        def rows(name, count=1, tag=None):
+            return keep.tile([P, count, V], F32, name=name, tag=tag or name, align_bytes=64)
+
+        att = [rows("att%d" % m, RANKS) for m in range(BLOCKS)]
+        step = [rows("step%d" % m, RANKS) for m in range(BLOCKS)]
+        chain = [rows("chain%d" % m, 2) for m in range(BLOCKS)]
+        second = [[rows("second%d%d" % (m, d)) for d in range(2)] for m in range(BLOCKS)]
+        pairs = [rows("pairs%d" % m, 2) for m in range(BLOCKS)]
+        below = [rows("below%d" % m) for m in range(BLOCKS)]
+        lower = [rows("lower%d" % m) for m in range(BLOCKS)]
+        clicks = [rows("clicks%d" % m) for m in range(BLOCKS)]
+        sat, both, inverse = {}, {}, {}
+
         def load_scales():
             for q in range(4):
-                (nc.sync, nc.scalar, nc.sync, nc.scalar)[q].dma_start(
+                (nc.sync, nc.scalar)[q % 2].dma_start(
                     scale_table[32 * q : 32 * q + 8, :].bitcast(I32),
                     x_scales[:, 4 * q : 4 * q + 4, :].bitcast(I32),
                 )
-
-
-        word_table, raw, ranks = {}, {}, []
-        g = keep.tile([P, V], F32, name="g")
 
         def load_words(o):
             word_table[o] = keep.tile([P, T], I32, name="word_table%d" % o, align_bytes=64)
@@ -53,236 +71,192 @@ def tile_picked_ydbnclk_sum_p_kernel(tc, x_words, x_scales, w1, w2, gam, offs, r
 
         def load_weights(i, o, m):
             raw[i, o, m] = keep.tile([P, PACK, P], F32, name="raw%d%d%d" % (i, o, m), align_bytes=64)
-            rows = (w1, w2)[i][512 * o : 512 * (o + 1), m * P : (m + 1) * P]
-            nc.sync.dma_start(raw[i, o, m][:], rows.rearrange("(p j) c -> p j c", j=PACK))
-
-        def load_rank(rk):
-            rank = lists.tile([P, V // 16], U16, name="rank%d" % len(ranks))
-            nc.sync.dma_start(rank[:], rk)
-            ranks.append(rank)
-
-        x_code, grouped, w_code, w_scale, banks, tables = {}, {}, {}, {}, {}, {}
-        x_scale = keep.tile([P, S], U8, name="x_scale", align_bytes=64)
-
-        def pick_scales():
-            nc.vector.tensor_copy(x_scale[:], scale_table[:].indirect(picks[:]))
+            part = (w1, w2)[i][K_PASS * o : K_PASS * (o + 1), m * P : (m + 1) * P]
+            nc.sync.dma_start(raw[i, o, m][:], part.rearrange("(p j) c -> p j c", j=PACK))
 
         def pick_words(o, a, b, tag):
             x_code[o, a] = keep.tile([P, b - a], U32, name="x_code%d_%d" % (o, a), tag=tag, align_bytes=64)
-            nc.vector.tensor_copy(x_code[o, a][:], word_table[o][:].bitcast(U32).indirect(picks[:, a // 16 : b // 16]))
+            offsets = picks[:, a // LIST_ROWS : b // LIST_ROWS]
+            nc.vector.tensor_copy(x_code[o, a][:], word_table[o][:].bitcast(U32).indirect(offsets))
 
-        def cast(i, o, m, by):
+        def cast(i, o, m, copy):
             grouped[i, o, m] = keep.tile([P, P * PACK], BF16, name="grouped%d%d%d" % (i, o, m), align_bytes=64)
-            dst = grouped[i, o, m][:].rearrange("p (c i t) -> p c t i", i=4, t=PACK)
-            src = raw[i, o, m][:].rearrange("p t (c i) -> p c t i", i=4)
-            if by == "v":
-                nc.vector.tensor_copy(dst, src)
-            else:
-                nc.scalar.copy(dst, src)
+            copy(
+                grouped[i, o, m][:].rearrange("p (c n t) -> p c t n", n=4, t=PACK),
+                raw[i, o, m][:].rearrange("p t (c n) -> p c t n", n=4),
+            )
 
         def quantize(i, o, m):
             w_code[i, o, m] = keep.tile([P, P], U32, name="w_code%d%d%d" % (i, o, m), align_bytes=64)
             w_scale[i, o, m] = keep.tile([P, P], U8, name="w_scale%d%d%d" % (i, o, m), align_bytes=64)
             nc.vector.quantize_mx(out=w_code[i, o, m][:].bitcast(FP8X4), scales=w_scale[i, o, m][:], in_=grouped[i, o, m][:])
 
-        def multiply(i, o, m, a, b, code, tag):
+        def multiply(i, o, m, a, b, tag=None):
             if o == 0:
                 banks[i, m, a] = psum.tile([P, b - a], F32, name="bank%d%d_%d" % (i, m, a), tag=tag)
+            first = a // BANK * BANK if o == 0 else a
             nc.tensor.matmul_mx(
                 out=banks[i, m, a][:],
                 lhsT=w_code[i, o, m][:].bitcast(FP8X4),
                 lhsT_scale=w_scale[i, o, m][:],
-                rhs=x_code[o, code][:, a - code : b - code].bitcast(FP8X4),
+                rhs=x_code[o, first][:, a - first : b - first].bitcast(FP8X4),
                 rhs_scale=x_scale[4 * o : P, a:b],
                 start=(o == 0),
                 stop=(o == PASSES - 1),
             )
 
-        def evacuate(i, m, a, b, by, tag=None):
-            if (i, m) not in tables:
-                tables[i, m] = keep.tile([P, S], F32, name="table%d%d" % (i, m), tag=tag or "table%d%d" % (i, m), align_bytes=64)
-            dst = tables[i, m][:, a:b]
-            if by == "sigmoid":
-                nc.scalar.activation(dst, banks[i, m, a][:], ACT.Sigmoid)
-            elif by == "v":
-                nc.vector.tensor_copy(dst, banks[i, m, a][:])
-            else:
-                nc.scalar.copy(dst, banks[i, m, a][:])
+        def new_table(i, m, tag=None):
+            name = "table%d%d" % (i, m)
+            tables[i, m] = keep.tile([P, S], F32, name=name, tag=tag or name, align_bytes=64)
 
-        def row(name, count=1, tag=None):
-            return keep.tile([P, count, V], F32, name=name, tag=tag or name, align_bytes=64)
+        def sigmoid(dst, src):
+            nc.scalar.activation(dst, src, ACT.Sigmoid)
 
-        att = [row("att%d" % m, 4) for m in range(TILES)]
-        sat = [row("sat%d" % m, 4) for m in range(TILES)]
-        both = {}
-        step = [row("step%d" % m, 4) for m in range(TILES)]
-        pair = [row("pair%d" % m, 2) for m in range(TILES)]
-        lost = [[row("lost%d%d" % (m, d)) for d in range(2)] for m in range(TILES)]
-        half = [row("half%d" % m, 2) for m in range(TILES)]
-        last = [row("last%d" % m) for m in range(TILES)]
-        square = [row("square%d" % m) for m in range(TILES)]
-        low = [row("low%d" % m) for m in range(TILES)]
-        clicks = [row("clicks%d" % m) for m in range(TILES)]
-        inverse = {}
+        def at_rank(i, m, r):
+            return tables[i, m][:].indirect(ranks[r][:])
 
         def fetch_att(m, r):
-            nc.scalar.activation(att[m][:, r, :], tables[0, m][:].indirect(ranks[r][:]), ACT.Sigmoid)
+            sigmoid(att[m][:, r, :], at_rank(ATT, m, r))
 
         def fetch_sat(m, r):
-            nc.scalar.activation(sat[m][:, r, :], tables[1, m][:].indirect(ranks[r][:]), ACT.Sigmoid)
-
-        def both_tile(m, a, b, tag):
-            tile = row("both%d%d" % (m, a), b - a, tag)
-            both[m, a, b] = tile[:]
-            for r in range(a, b):
-                both[m, r] = tile[:, r - a, :]
+            if r % 2 == 0:
+                sat[m, r // 2] = rows("sat%d%d" % (m, r // 2), 2)
+            sigmoid(sat[m, r // 2][:, r % 2, :], at_rank(SAT, m, r))
 
         def fetch_both(m, r):
-            nc.vector.tensor_tensor(both[m, r], tables[1, m][:].indirect(ranks[r][:]), att[m][:, r, :], ALU.mult)
+            nc.vector.tensor_tensor(both[m, r][:, 0, :], at_rank(SAT, m, r), att[m][:, r, :], ALU.mult)
 
-        def do_both(m, a, b):
-            nc.vector.tensor_tensor(both[m, a, b], sat[m][:, a:b, :], att[m][:, a:b, :], ALU.mult)
+        def do_both(m, a, b, tag):
+            both[m, a] = rows("both%d%d" % (m, a), b - a, tag)[:]
+            nc.vector.tensor_tensor(both[m, a], sat[m, a // 2][:, a % 2 : a % 2 + b - a, :], att[m][:, a:b, :], ALU.mult)
 
-        def do_step(m, a, b):
-            nc.vector.scalar_tensor_tensor(
-                step[m][:, a:b, :], both[m, a, b], 1.0, g[:].unsqueeze(1).to_broadcast([P, b - a, V]), ALU.subtract, ALU.mult
-            )
+        def do_step(m, a, b, products):
+            factor = g[:].unsqueeze(1).to_broadcast([P, b - a, V])
+            nc.vector.scalar_tensor_tensor(step[m][:, a:b, :], products, 1.0, factor, ALU.subtract, ALU.mult)
 
-        def warm_up(ap):
-            warm = keep.tile([P, 1], F32, name="warm")
-            nc.scalar.activation(warm[:], ap, ACT.Sigmoid)
+        def do_second(m, d):
+            nc.vector.tensor_tensor(second[m][d][:, 0, :], step[m][:, 2 * d, :], att[m][:, 2 * d + 1, :], ALU.mult)
+
+        def do_chain(m):
+            nc.vector.tensor_tensor(chain[m][:, 0, :], step[m][:, 0, :], step[m][:, 1, :], ALU.mult)
 
         def do_pair(m, d):
-            nc.vector.tensor_tensor(pair[m][:, d, :], step[m][:, 2 * d, :], step[m][:, 2 * d + 1, :], ALU.mult)
+            nc.vector.tensor_tensor(pairs[m][:, d, :], att[m][:, 2 * d, :], second[m][d][:, 0, :], ALU.subtract)
 
-        def do_lost(m, d):
-            nc.vector.tensor_tensor(lost[m][d][:, 0, :], step[m][:, 2 * d, :], att[m][:, 2 * d + 1, :], ALU.mult)
-
-        def do_half(m, d):
-            nc.vector.tensor_tensor(half[m][:, d, :], att[m][:, 2 * d, :], lost[m][d][:, 0, :], ALU.subtract)
-
-        def wide(fn_out, fn_a, fn_b, op):
-            nc.vector.tensor_tensor(fn_out, fn_a, fn_b, op)
-
-        def do_last(m):
-            nc.vector.tensor_tensor(last[m][:, 0, :], pair[m][:, 0, :], pair[m][:, 1, :], ALU.mult)
-            nc.scalar.activation(square[m][:], last[m][:], ACT.Square, bias=1.0, scale=-0.5)
-
-        def do_low(m):
-            nc.vector.tensor_tensor(low[m][:, 0, :], half[m][:, 1, :], pair[m][:, 0, :], ALU.mult)
+        def do_lower_ranks(m):
+            nc.vector.tensor_tensor(chain[m][:, 1, :], chain[m][:, 0, :], step[m][:, 2, :], ALU.mult)
+            do_second(m, 1)
+            nc.vector.tensor_tensor(step[m][:, 3, :], chain[m][:, 1, :], g[:], ALU.mult)
+            do_pair(m, 1)
+            nc.vector.scalar_tensor_tensor(below[m][:, 0, :], both[m, 3][:, 0, :], 1.0, step[m][:, 3, :], ALU.subtract, ALU.mult)
+            nc.vector.tensor_tensor(lower[m][:, 0, :], pairs[m][:, 1, :], chain[m][:, 0, :], ALU.mult)
 
         def do_clicks(m):
-            nc.vector.tensor_tensor(clicks[m][:, 0, :], low[m][:, 0, :], half[m][:, 0, :], ALU.add)
+            nc.vector.tensor_tensor(clicks[m][:, 0, :], lower[m][:, 0, :], pairs[m][:, 0, :], ALU.add)
 
-        def do_inverse(m, tag):
-            inverse[m] = row("inverse%d" % m, 1, tag)
-            nc.scalar.activation(inverse[m][:], square[m][:], ACT.Abs_reciprocal_sqrt)
+        def do_inverse(m, tag=None):
+            square = rows("square%d" % m, 1, tag)
+            nc.scalar.activation(square[:], below[m][:], ACT.Square, bias=1.0, scale=-0.5)
+            inverse[m] = rows("inverse%d" % m)
+            nc.scalar.activation(inverse[m][:], square[:], ACT.Abs_reciprocal_sqrt)
 
-        def finish(m, queue, tag):
-            result = row("result%d" % m, 1, tag)
+        def finish(m, tag=None):
+            result = rows("result%d" % m, 1, tag)
             nc.vector.tensor_tensor(result[:], clicks[m][:], inverse[m][:], ALU.mult)
-            queue.dma_start(out[m * P : (m + 1) * P, :], result[:, 0, :])
+            nc.sync.dma_start(out[m * P : (m + 1) * P, :], result[:, 0, :])
 
-        def clock(ap, name):
-            tick = keep.tile([P, 1], F32, name=name)
-            nc.gpsimd.tensor_copy(tick[:], ap)
-
-        load_weights(0, 0, 0)
+        load_weights(ATT, 0, 0)
         load_scales()
         load_words(0)
-        load_weights(1, 0, 0)
+        load_weights(SAT, 0, 0)
         load_words(1)
-        load_weights(0, 1, 0)
-        load_weights(1, 1, 0)
-        for rk in (rk1, rk2, rk3, rk4):
-            load_rank(rk)
-        for i in range(2):
+        load_weights(ATT, 1, 0)
+        load_weights(SAT, 1, 0)
+        for r, rk in enumerate((rk1, rk2, rk3, rk4)):
+            ranks.append(lists.tile([P, V // LIST_ROWS], U16, name="rank%d" % r))
+            nc.sync.dma_start(ranks[r][:], rk)
+        for i in (ATT, SAT):
             for o in range(PASSES):
                 load_weights(i, o, 1)
         nc.sync.dma_start(g[:], gam)
 
-        warm_up(raw[0, 0, 0][:, 0, 0:1])
-        pick_scales()
-        pick_words(0, 0, 512, "x00")
-        pick_words(0, 512, 1024, "x01")
+        warm = keep.tile([P, 1], F32, name="warm")
+        sigmoid(warm[:], raw[ATT, 0, 0][:, 0, 0:1])
+
+        nc.vector.tensor_copy(x_scale[:], scale_table[:].indirect(picks[:]))
+        for a in range(0, S, BANK):
+            pick_words(0, a, a + BANK, "x_code0_%d" % a)
         for o in range(PASSES):
-            for i in range(2):
-                cast(i, o, 0, "s")
-        quantize(0, 0, 0)
-        quantize(1, 0, 0)
-        pick_words(1, 0, 512, "x10")
-        quantize(0, 1, 0)
-        pick_words(1, 512, 768, "grouped010")
-        quantize(1, 1, 0)
-        pick_words(1, 768, 1024, "grouped110")
-        CUTS = ((0, 512), (512, 768), (768, 1024))
-        for i in range(2):
+            for i in (ATT, SAT):
+                cast(i, o, 0, nc.scalar.copy)
+        quantize(ATT, 0, 0)
+        quantize(SAT, 0, 0)
+        pick_words(1, *CUTS[0], "x_code1_0")
+        quantize(ATT, 1, 0)
+        pick_words(1, *CUTS[1], "grouped010")
+        quantize(SAT, 1, 0)
+        pick_words(1, *CUTS[2], "grouped110")
+        for i in (ATT, SAT):
             for a, b in CUTS:
-                multiply(i, 0, 0, a, b, a // 512 * 512, "bank%d_%d" % (i, a))
+                multiply(i, 0, 0, a, b, "bank%d_%d" % (i, a))
         for a, b in CUTS:
-            for i in range(2):
-                multiply(i, 1, 0, a, b, a, None)
-        cast(0, 0, 1, "s")
-        cast(0, 1, 1, "s")
-        quantize(0, 0, 1)
-        cast(1, 0, 1, "v")
-        quantize(0, 1, 1)
+            for i in (ATT, SAT):
+                multiply(i, 1, 0, a, b)
+
+        cast(ATT, 0, 1, nc.scalar.copy)
+        cast(ATT, 1, 1, nc.scalar.copy)
+        quantize(ATT, 0, 1)
+        cast(SAT, 0, 1, nc.vector.tensor_copy)
+        quantize(ATT, 1, 1)
+        new_table(ATT, 0, "raw101")
+        new_table(SAT, 0, "raw011")
         for a, b in CUTS:
-            evacuate(0, 0, a, b, "v", "raw101")
-            evacuate(1, 0, a, b, "sigmoid", "raw011")
-        cast(1, 1, 1, "v")
-        quantize(1, 0, 1)
-        quantize(1, 1, 1)
-        for r in range(4):
+            nc.vector.tensor_copy(tables[ATT, 0][:, a:b], banks[ATT, 0, a][:])
+            sigmoid(tables[SAT, 0][:, a:b], banks[SAT, 0, a][:])
+        cast(SAT, 1, 1, nc.vector.tensor_copy)
+        quantize(SAT, 0, 1)
+        quantize(SAT, 1, 1)
+        for r in range(RANKS):
             fetch_att(0, r)
-        TAGS = (("fresh0", "bank0_0", "bank0_512"), ("fresh1", "bank1_0", "bank1_512"))
-        for i in range(2):
-            for c, (a, b) in enumerate(CUTS):
-                multiply(i, 0, 1, a, b, a // 512 * 512, TAGS[i][c])
-                multiply(i, 1, 1, a, b, a, None)
-        for i in range(2):
+
+        for i in (ATT, SAT):
+            for tag, (a, b) in zip(("spare%d" % i, "bank%d_%d" % (i, 0), "bank%d_%d" % (i, BANK)), CUTS):
+                multiply(i, 0, 1, a, b, tag)
+                multiply(i, 1, 1, a, b)
+        for i in (ATT, SAT):
+            new_table(i, 1)
             for a, b in CUTS:
-                evacuate(i, 1, a, b, "s")
-        both_tile(0, 0, 4, "grouped111")
-        both[0, 0, 2] = both[0, 0, 4][:, 0:2, :]
-        both[0, 2, 4] = both[0, 0, 4][:, 2:4, :]
-        fetch_both(0, 0)
-        fetch_both(0, 1)
-        fetch_both(0, 2)
-        do_step(0, 0, 2)
+                nc.scalar.copy(tables[i, 1][:, a:b], banks[i, 1, a][:])
+
+        products = rows("both00", RANKS, "grouped111")
+        for r in range(RANKS):
+            both[0, r] = products[:, r : r + 1, :]
+        for r in range(3):
+            fetch_both(0, r)
+        do_step(0, 0, 2, products[:, 0:2, :])
         fetch_both(0, 3)
-        do_lost(0, 0)
-        do_step(0, 2, 4)
+        do_second(0, 0)
+        do_step(0, 2, 3, both[0, 2])
+        do_chain(0)
         do_pair(0, 0)
-        do_half(0, 0)
-        do_lost(0, 1)
-        do_pair(0, 1)
-        do_half(0, 1)
-        do_last(0)
-        do_low(0)
-        for r in range(4):
+        do_lower_ranks(0)
+
+        for r in range(RANKS):
             fetch_att(1, r)
             fetch_sat(1, r)
-        both_tile(1, 0, 2, "step0")
-        do_both(1, 0, 2)
+        do_both(1, 0, 2, "second01")
         do_clicks(0)
-        do_step(1, 0, 2)
-        both_tile(1, 2, 3, "step0")
-        do_both(1, 2, 3)
-        do_lost(1, 0)
+        do_step(1, 0, 2, both[1, 0])
+        do_second(1, 0)
+        do_chain(1)
+        do_both(1, 2, 3, "second01")
         do_pair(1, 0)
-        do_step(1, 2, 3)
-        do_half(1, 0)
-        both_tile(1, 3, 4, "lost10")
-        do_both(1, 3, 4)
-        do_lost(1, 1)
-        do_step(1, 3, 4)
+        do_step(1, 2, 3, both[1, 2])
+        do_both(1, 3, 4, "second10")
+        do_lower_ranks(1)
+
         do_inverse(0, "table11")
-        do_pair(1, 1)
-        do_half(1, 1)
-        do_last(1)
-        finish(0, nc.sync, "step1")
-        do_low(1)
+        finish(0, "step1")
         do_clicks(1)
-        do_inverse(1, None)
-        finish(1, nc.sync, None)
+        do_inverse(1)
+        finish(1)

from contextlib import ExitStack

import concourse.mybir as mybir

F32 = mybir.dt.float32
BF16 = mybir.dt.bfloat16
I32 = mybir.dt.int32
U32 = mybir.dt.uint32
U16 = mybir.dt.uint16
U8 = mybir.dt.uint8
FP8X4 = mybir.dt.float8_e4m3fn_x4
ACT = mybir.ActivationFunctionType
ALU = mybir.AluOpType

K, T, S, N, V = 1024, 2048, 1024, 256, 256
P = 128
PACK = 4
K_PASS = P * PACK
PASSES = K // K_PASS
BLOCKS = N // P
RANKS = 4
LIST_ROWS = 16
ATT, SAT = 0, 1
BANK = 512
CUTS = ((0, BANK), (BANK, BANK + BANK // 2), (BANK + BANK // 2, S))
FLOPS = 2 * 2 * K * N * S


def tile_picked_ydbnclk_sum_p_kernel(tc, x_words, x_scales, w1, w2, gam, offs, rk1, rk2, rk3, rk4, out):
    nc = tc.nc
    with ExitStack() as ctx:
        lists = ctx.enter_context(tc.tile_pool(name="lists", bufs=1))
        keep = ctx.enter_context(tc.tile_pool(name="keep", bufs=1))
        psum = ctx.enter_context(tc.psum_pool(name="psum", bufs=1))

        picks = lists.tile([P, S // LIST_ROWS], U16, name="picks")
        nc.sync.dma_start(picks[:], offs)

        scale_table = keep.tile([P, T], U8, name="scale_table", align_bytes=64)
        nc.vector.memset(scale_table[:, : T // 2].bitcast(I32), 0)
        nc.gpsimd.memset(scale_table[:, T // 2 :].bitcast(I32), 0)

        g = keep.tile([P, V], F32, name="g")
        x_scale = keep.tile([P, S], U8, name="x_scale", align_bytes=64)
        word_table, raw, ranks = {}, {}, []
        x_code, grouped, w_code, w_scale, banks, tables = {}, {}, {}, {}, {}, {}

        def rows(name, count=1, tag=None):
            return keep.tile([P, count, V], F32, name=name, tag=tag or name, align_bytes=64)

        att = [rows("att%d" % m, RANKS) for m in range(BLOCKS)]
        step = [rows("step%d" % m, RANKS) for m in range(BLOCKS)]
        chain = [rows("chain%d" % m, 2) for m in range(BLOCKS)]
        second = [[rows("second%d%d" % (m, d)) for d in range(2)] for m in range(BLOCKS)]
        pairs = [rows("pairs%d" % m, 2) for m in range(BLOCKS)]
        below = [rows("below%d" % m) for m in range(BLOCKS)]
        lower = [rows("lower%d" % m) for m in range(BLOCKS)]
        clicks = [rows("clicks%d" % m) for m in range(BLOCKS)]
        sat, both, inverse = {}, {}, {}

        def load_scales():
            for q in range(4):
                (nc.sync, nc.scalar)[q % 2].dma_start(
                    scale_table[32 * q : 32 * q + 8, :].bitcast(I32),
                    x_scales[:, 4 * q : 4 * q + 4, :].bitcast(I32),
                )

        def load_words(o):
            word_table[o] = keep.tile([P, T], I32, name="word_table%d" % o, align_bytes=64)
            nc.sync.dma_start(word_table[o][:], x_words[o].rearrange("p n t -> p (n t)").bitcast(I32))

        def load_weights(i, o, m):
            raw[i, o, m] = keep.tile([P, PACK, P], F32, name="raw%d%d%d" % (i, o, m), align_bytes=64)
            part = (w1, w2)[i][K_PASS * o : K_PASS * (o + 1), m * P : (m + 1) * P]
            nc.sync.dma_start(raw[i, o, m][:], part.rearrange("(p j) c -> p j c", j=PACK))

        def pick_words(o, a, b, tag):
            x_code[o, a] = keep.tile([P, b - a], U32, name="x_code%d_%d" % (o, a), tag=tag, align_bytes=64)
            offsets = picks[:, a // LIST_ROWS : b // LIST_ROWS]
            nc.vector.tensor_copy(x_code[o, a][:], word_table[o][:].bitcast(U32).indirect(offsets))

        def cast(i, o, m, copy):
            grouped[i, o, m] = keep.tile([P, P * PACK], BF16, name="grouped%d%d%d" % (i, o, m), align_bytes=64)
            copy(
                grouped[i, o, m][:].rearrange("p (c n t) -> p c t n", n=4, t=PACK),
                raw[i, o, m][:].rearrange("p t (c n) -> p c t n", n=4),
            )

        def quantize(i, o, m):
            w_code[i, o, m] = keep.tile([P, P], U32, name="w_code%d%d%d" % (i, o, m), align_bytes=64)
            w_scale[i, o, m] = keep.tile([P, P], U8, name="w_scale%d%d%d" % (i, o, m), align_bytes=64)
            nc.vector.quantize_mx(out=w_code[i, o, m][:].bitcast(FP8X4), scales=w_scale[i, o, m][:], in_=grouped[i, o, m][:])

        def multiply(i, o, m, a, b, tag=None):
            if o == 0:
                banks[i, m, a] = psum.tile([P, b - a], F32, name="bank%d%d_%d" % (i, m, a), tag=tag)
            first = a // BANK * BANK if o == 0 else a
            nc.tensor.matmul_mx(
                out=banks[i, m, a][:],
                lhsT=w_code[i, o, m][:].bitcast(FP8X4),
                lhsT_scale=w_scale[i, o, m][:],
                rhs=x_code[o, first][:, a - first : b - first].bitcast(FP8X4),
                rhs_scale=x_scale[4 * o : P, a:b],
                start=(o == 0),
                stop=(o == PASSES - 1),
            )

        def new_table(i, m, tag=None):
            name = "table%d%d" % (i, m)
            tables[i, m] = keep.tile([P, S], F32, name=name, tag=tag or name, align_bytes=64)

        def sigmoid(dst, src):
            nc.scalar.activation(dst, src, ACT.Sigmoid)

        def at_rank(i, m, r):
            return tables[i, m][:].indirect(ranks[r][:])

        def fetch_att(m, r):
            sigmoid(att[m][:, r, :], at_rank(ATT, m, r))

        def fetch_sat(m, r):
            if r % 2 == 0:
                sat[m, r // 2] = rows("sat%d%d" % (m, r // 2), 2)
            sigmoid(sat[m, r // 2][:, r % 2, :], at_rank(SAT, m, r))

        def fetch_both(m, r):
            nc.vector.tensor_tensor(both[m, r][:, 0, :], at_rank(SAT, m, r), att[m][:, r, :], ALU.mult)

        def do_both(m, a, b, tag):
            both[m, a] = rows("both%d%d" % (m, a), b - a, tag)[:]
            nc.vector.tensor_tensor(both[m, a], sat[m, a // 2][:, a % 2 : a % 2 + b - a, :], att[m][:, a:b, :], ALU.mult)

        def do_step(m, a, b, products):
            factor = g[:].unsqueeze(1).to_broadcast([P, b - a, V])
            nc.vector.scalar_tensor_tensor(step[m][:, a:b, :], products, 1.0, factor, ALU.subtract, ALU.mult)

        def do_second(m, d):
            nc.vector.tensor_tensor(second[m][d][:, 0, :], step[m][:, 2 * d, :], att[m][:, 2 * d + 1, :], ALU.mult)

        def do_chain(m):
            nc.vector.tensor_tensor(chain[m][:, 0, :], step[m][:, 0, :], step[m][:, 1, :], ALU.mult)

        def do_pair(m, d):
            nc.vector.tensor_tensor(pairs[m][:, d, :], att[m][:, 2 * d, :], second[m][d][:, 0, :], ALU.subtract)

        def do_lower_ranks(m):
            nc.vector.tensor_tensor(chain[m][:, 1, :], chain[m][:, 0, :], step[m][:, 2, :], ALU.mult)
            do_second(m, 1)
            nc.vector.tensor_tensor(step[m][:, 3, :], chain[m][:, 1, :], g[:], ALU.mult)
            do_pair(m, 1)
            nc.vector.scalar_tensor_tensor(below[m][:, 0, :], both[m, 3][:, 0, :], 1.0, step[m][:, 3, :], ALU.subtract, ALU.mult)
            nc.vector.tensor_tensor(lower[m][:, 0, :], pairs[m][:, 1, :], chain[m][:, 0, :], ALU.mult)

        def do_clicks(m):
            nc.vector.tensor_tensor(clicks[m][:, 0, :], lower[m][:, 0, :], pairs[m][:, 0, :], ALU.add)

        def do_inverse(m, tag=None):
            square = rows("square%d" % m, 1, tag)
            nc.scalar.activation(square[:], below[m][:], ACT.Square, bias=1.0, scale=-0.5)
            inverse[m] = rows("inverse%d" % m)
            nc.scalar.activation(inverse[m][:], square[:], ACT.Abs_reciprocal_sqrt)

        def finish(m, tag=None):
            result = rows("result%d" % m, 1, tag)
            nc.vector.tensor_tensor(result[:], clicks[m][:], inverse[m][:], ALU.mult)
            nc.sync.dma_start(out[m * P : (m + 1) * P, :], result[:, 0, :])

        load_weights(ATT, 0, 0)
        load_scales()
        load_words(0)
        load_weights(SAT, 0, 0)
        load_words(1)
        load_weights(ATT, 1, 0)
        load_weights(SAT, 1, 0)
        for r, rk in enumerate((rk1, rk2, rk3, rk4)):
            ranks.append(lists.tile([P, V // LIST_ROWS], U16, name="rank%d" % r))
            nc.sync.dma_start(ranks[r][:], rk)
        for i in (ATT, SAT):
            for o in range(PASSES):
                load_weights(i, o, 1)
        nc.sync.dma_start(g[:], gam)

        warm = keep.tile([P, 1], F32, name="warm")
        sigmoid(warm[:], raw[ATT, 0, 0][:, 0, 0:1])

        nc.vector.tensor_copy(x_scale[:], scale_table[:].indirect(picks[:]))
        for a in range(0, S, BANK):
            pick_words(0, a, a + BANK, "x_code0_%d" % a)
        for o in range(PASSES):
            for i in (ATT, SAT):
                cast(i, o, 0, nc.scalar.copy)
        quantize(ATT, 0, 0)
        quantize(SAT, 0, 0)
        pick_words(1, *CUTS[0], "x_code1_0")
        quantize(ATT, 1, 0)
        pick_words(1, *CUTS[1], "grouped010")
        quantize(SAT, 1, 0)
        pick_words(1, *CUTS[2], "grouped110")
        for i in (ATT, SAT):
            for a, b in CUTS:
                multiply(i, 0, 0, a, b, "bank%d_%d" % (i, a))
        for a, b in CUTS:
            for i in (ATT, SAT):
                multiply(i, 1, 0, a, b)

        cast(ATT, 0, 1, nc.scalar.copy)
        cast(ATT, 1, 1, nc.scalar.copy)
        quantize(ATT, 0, 1)
        cast(SAT, 0, 1, nc.vector.tensor_copy)
        quantize(ATT, 1, 1)
        new_table(ATT, 0, "raw101")
        new_table(SAT, 0, "raw011")
        for a, b in CUTS:
            nc.vector.tensor_copy(tables[ATT, 0][:, a:b], banks[ATT, 0, a][:])
            sigmoid(tables[SAT, 0][:, a:b], banks[SAT, 0, a][:])
        cast(SAT, 1, 1, nc.vector.tensor_copy)
        quantize(SAT, 0, 1)
        quantize(SAT, 1, 1)
        for r in range(RANKS):
            fetch_att(0, r)

        for i in (ATT, SAT):
            for tag, (a, b) in zip(("spare%d" % i, "bank%d_%d" % (i, 0), "bank%d_%d" % (i, BANK)), CUTS):
                multiply(i, 0, 1, a, b, tag)
                multiply(i, 1, 1, a, b)
        for i in (ATT, SAT):
            new_table(i, 1)
            for a, b in CUTS:
                nc.scalar.copy(tables[i, 1][:, a:b], banks[i, 1, a][:])

        products = rows("both00", RANKS, "grouped111")
        for r in range(RANKS):
            both[0, r] = products[:, r : r + 1, :]
        for r in range(3):
            fetch_both(0, r)
        do_step(0, 0, 2, products[:, 0:2, :])
        fetch_both(0, 3)
        do_second(0, 0)
        do_step(0, 2, 3, both[0, 2])
        do_chain(0)
        do_pair(0, 0)
        do_lower_ranks(0)

        for r in range(RANKS):
            fetch_att(1, r)
            fetch_sat(1, r)
        do_both(1, 0, 2, "second01")
        do_clicks(0)
        do_step(1, 0, 2, both[1, 0])
        do_second(1, 0)
        do_chain(1)
        do_both(1, 2, 3, "second01")
        do_pair(1, 0)
        do_step(1, 2, 3, both[1, 2])
        do_both(1, 3, 4, "second10")
        do_lower_ranks(1)

        do_inverse(0, "table11")
        finish(0, "step1")
        do_clicks(1)
        do_inverse(1)
        finish(1)
